import numpy as np
import ml_dtypes


def mxq(x, axis, fmt="e4m3"):
    dtype, down = {"e4m3": (ml_dtypes.float8_e4m3fn, 7), "e5m2": (ml_dtypes.float8_e5m2, 14)}[fmt]
    v = np.moveaxis(np.asarray(x, np.float32).astype(ml_dtypes.bfloat16).astype(np.float64), axis, -1)
    blocks = v.reshape(v.shape[:-1] + (-1, 32))
    amax = np.abs(blocks).max(-1, keepdims=True)
    byte = np.maximum(np.where(amax > 0, np.frexp(amax)[1] - 1 + 127, 0) - down, 1)
    scale = np.exp2(byte - 127.0)
    codes = (blocks / scale).astype(np.float32).astype(dtype).astype(np.float64)
    return np.moveaxis((codes * scale).reshape(v.shape), -1, axis)


WIDE = False


def mx_kscale(k):
    if not WIDE:
        return np.ones(k)
    levels = np.array([10, -10, 5, -5, 0])
    if k % 512:
        return np.exp2(np.random.permutation(np.resize(levels, k // 32))).repeat(32)
    a = np.empty((k // 512, 16))
    for p in range(k // 512):
        a[p, :8] = np.random.permutation(np.resize(levels, 8))
        for g in range(8):
            far = levels[np.abs(levels - a[p, g]) >= 10]
            a[p, g + 8] = far[np.random.randint(len(far))]
    return np.exp2(a.ravel()).repeat(32)


def f64(x):
    return np.asarray(x).astype(np.float64)


def striped(idx):
    return np.tile(idx.reshape(-1, 16).T, (8, 1)).astype(np.uint16)


def unstriped(offs):
    return offs[:16].T.reshape(-1).astype(np.int64)


E2M1 = np.array([0.0, 0.5, 1.0, 1.5, 2.0, 3.0, 4.0, 6.0, -0.0, -0.5, -1.0, -1.5, -2.0, -3.0, -4.0, -6.0])


def pack_weight(w, fmt):
    k, n = w.shape
    w = f64(np.asarray(w, np.float32).astype(ml_dtypes.bfloat16)).reshape(k // 32, 32, n)
    amax = np.abs(w).max(1)
    if fmt == "e4m3":
        byte = np.frexp(amax)[1] - 1 + 127 - 7
    else:
        mant, ex = np.frexp(amax / 6.0)
        byte = np.where(mant > 0.5, ex, ex - 1) + 127
    byte = np.clip(np.where(amax > 0, byte, 1), 1, 254)
    scaled = (w * np.exp2(127.0 - byte)[:, None, :]).reshape(k, n).astype(np.float32)
    by_word = np.ascontiguousarray(scaled.reshape(k // 512, 128, 4, n).transpose(0, 1, 3, 2))
    if fmt == "e4m3":
        words = by_word.astype(ml_dtypes.float8_e4m3fn).view(np.uint8)
    else:
        c = by_word.astype(ml_dtypes.float4_e2m1fn).view(np.uint8) & 0xF
        words = (c[..., 0::2] | (c[..., 1::2] << 4)).reshape(k // 512, 128, 2 * n)
    return np.ascontiguousarray(words), np.ascontiguousarray(byte.astype(np.uint8).reshape(k // 512, 16, n))


def unpack_weight(words, scales, fmt):
    g, _, n = scales.shape
    words = np.ascontiguousarray(words).reshape(g, 128, n, -1)
    if fmt == "e4m3":
        vals = words.view(ml_dtypes.float8_e4m3fn).astype(np.float64)
    else:
        nib = np.empty((g, 128, n, 4), np.uint8)
        nib[..., 0::2] = words & 0xF
        nib[..., 1::2] = words >> 4
        vals = E2M1[nib]
    vals = vals * np.repeat(np.exp2(scales.astype(np.float64) - 127.0), 8, axis=1)[..., None]
    return vals.transpose(0, 1, 3, 2).reshape(g * 512, n)


def gelu(v):
    return 0.5 * v * (1.0 + np.tanh(np.sqrt(2.0 / np.pi) * (v + 0.044715 * v**3)))


K, H, T, S, T3, S2 = 1536, 1024, 2048, 512, 2048, 512

def setup_inputs():
    n = np.random.standard_normal
    s = mx_kscale(K)[:, None]
    u = mx_kscale(H)[:, None]
    tab_words, tab_scales = pack_weight(n((K, T)) * s, "e4m3")
    tab2_words, tab2_scales = pack_weight(1.4 * n((H, T3)) / np.sqrt(H) / u, "e4m3")
    tab3_words, tab3_scales = pack_weight(n((H, T3)) / np.sqrt(H) / u, "e4m3")
    w1 = (n((K, H)) / np.sqrt(K) / s * u.T).astype(np.float32)
    w4_words, w4_scales = pack_weight(n((K, H)) / np.sqrt(K) / s * u.T, "e2m1")
    steep = (1.2 * np.exp(0.5 * n(S2))).astype(np.float32)
    offs = striped(np.random.permutation(T)[:S])
    offs2 = striped(np.random.permutation(T3)[:S2])
    offs3 = striped(np.random.permutation(T3)[:S2])
    return dict(tab_words=tab_words, tab_scales=tab_scales, tab2_words=tab2_words, tab2_scales=tab2_scales,
                tab3_words=tab3_words, tab3_scales=tab3_scales, w1=w1, w4_words=w4_words, w4_scales=w4_scales,
                steep=steep, offs=offs, offs2=offs2, offs3=offs3)

def reference(tab_words, tab_scales, tab2_words, tab2_scales, tab3_words, tab3_scales,
              w1, w4_words, w4_scales, steep, offs, offs2, offs3):
    v = unpack_weight(tab_words, tab_scales, "e4m3")[:, unstriped(offs)]
    v2 = unpack_weight(tab2_words, tab2_scales, "e4m3")[:, unstriped(offs2)]
    v3 = unpack_weight(tab3_words, tab3_scales, "e4m3")[:, unstriped(offs3)]
    w4 = unpack_weight(w4_words, w4_scales, "e2m1")
    h1 = mxq(f64(w1), 0, "e4m3").T @ v
    h2 = w4.T @ v
    h = mxq(np.maximum(h1, h2), 0, "e4m3")
    e2 = v2.T @ h
    e3 = v3.T @ h
    room = e2 / (1.0 + np.exp(-e2))
    mate = np.tanh(f64(steep)[:, None] * e3)
    return room + mate

@@ -1,0 +1,264 @@
+from contextlib import ExitStack
+
+import concourse.mybir as mybir
+from concourse.masks import make_identity
+
+K, H, T, S = 1536, 1024, 2048, 512
+FLOPS = 2 * (2 * K * H * S + 2 * H * S * S)
+
+F32 = mybir.dt.float32
+BF16 = mybir.dt.bfloat16
+I32 = mybir.dt.int32
+U32 = mybir.dt.uint32
+U16 = mybir.dt.uint16
+U8 = mybir.dt.uint8
+FP8X4 = mybir.dt.float8_e4m3fn_x4
+FP4X4 = mybir.dt.float4_e2m1fn_x4
+ACT = mybir.ActivationFunctionType
+ALU = mybir.AluOpType
+
+P = 128
+PACK = 4
+PASS = P * PACK
+K_PASSES = K // PASS
+H_PASSES = H // PASS
+TILES = S // P
+QUADS = 4
+HALF = S // 2
+
+
+def tile_list_flatshare_pair_ranking_kernel(
+    tc, tab_words, tab_scales, tab2_words, tab2_scales, tab3_words, tab3_scales,
+    w1, w4_words, w4_scales, steep, offs, offs2, offs3, out,
+):
+    nc = tc.nc
+    with ExitStack() as ctx:
+        keep = ctx.enter_context(tc.tile_pool(name="keep", bufs=1))
+        psum = ctx.enter_context(tc.psum_pool(name="psum", bufs=1))
+
+        def sb(name, shape, dtype):
+            return keep.tile(shape, dtype, name=name, align_bytes=64)
+
+        def ring(tag, bufs, name, shape, dtype):
+            return keep.tile(shape, dtype, name=name, tag=tag, bufs=bufs, align_bytes=64)
+
+        def bank(i, name):
+            return psum.tile([P, PASS], F32, name=name, tag="bank%d" % i)
+
+        def load_list(name, src):
+            lst = keep.tile([P, S // 16], U16, name=name)
+            nc.sync.dma_start(lst[:], src)
+            return lst
+
+        def load_words(name, words):
+            win = sb(name, [P, T], U32)
+            nc.sync.dma_start(win[:].bitcast(I32), words.rearrange("p t i -> p (t i)").bitcast(I32))
+            return win
+
+        def load_planes_side_by_side(plane, scales, passes):
+            for q in range(QUADS):
+                nc.sync.dma_start(
+                    plane[32 * q : 32 * q + 4, :].bitcast(I32).rearrange("r (a t) -> r a t", a=passes),
+                    scales.bitcast(I32)[:, 4 * q : 4 * q + 4, :].rearrange("a r t -> r a t"),
+                )
+
+        def load_planes_stacked(plane, scales, passes):
+            for q in range(QUADS):
+                nc.sync.dma_start(
+                    plane[32 * q : 32 * q + 4 * passes, :].bitcast(I32),
+                    scales.bitcast(I32)[:, 4 * q : 4 * q + 4, :],
+                )
+
+        def gather(name, dtype, window, offsets):
+            picked = sb(name, [P, S], dtype)
+            nc.vector.tensor_copy(picked[:], window.indirect(offsets[:]))
+            return picked
+
+        v_scale_win = sb("v_scale_win", [P, K_PASSES * T], U8)
+        w4_scale = sb("w4_scale", [P, K_PASSES * H], U8)
+        v2_scale_win = sb("v2_scale_win", [P, T], U8)
+        v3_scale_win = sb("v3_scale_win", [P, T], U8)
+        nc.vector.memset(v_scale_win[:].bitcast(I32), 0)
+        nc.vector.memset(w4_scale[:].bitcast(I32), 0)
+        nc.gpsimd.memset(v2_scale_win[:].bitcast(I32), 0)
+        nc.gpsimd.memset(v3_scale_win[:].bitcast(I32), 0)
+
+        idx = load_list("idx", offs)
+        v_win = [load_words("v_win0", tab_words[0])]
+        load_planes_side_by_side(v_scale_win, tab_scales, K_PASSES)
+        w4_codes = sb("w4_codes", [P, K_PASSES, 2 * H], U8)
+        nc.sync.dma_start(w4_codes[:].bitcast(I32), w4_words.bitcast(I32).rearrange("a p c -> p a c"))
+        load_planes_side_by_side(w4_scale, w4_scales, K_PASSES)
+        v_win.append(load_words("v_win1", tab_words[1]))
+        v_win.append(load_words("v_win2", tab_words[2]))
+        idx2 = load_list("idx2", offs2)
+        load_planes_stacked(v2_scale_win, tab2_scales, H_PASSES)
+
+        w1_raw = {}
+
+        def w1_rows(a):
+            return w1[a * PASS : (a + 1) * PASS, :].rearrange("(p i) c -> p i c", i=PACK)
+
+        raw = sb("w1_raw0", [P, PACK, H], F32)
+        nc.sync.dma_start(raw[:], w1_rows(0))
+        for b in range(H_PASSES):
+            w1_raw[0, b] = raw[:, :, b * PASS : (b + 1) * PASS]
+        idx3 = load_list("idx3", offs3)
+        load_planes_stacked(v3_scale_win, tab3_scales, H_PASSES)
+        steep_sb = keep.tile([P, TILES], F32, name="steep_sb")
+        with nc.allow_non_contiguous_dma(reason="one factor for each output row"):
+            nc.sync.dma_start(steep_sb[:], steep.rearrange("(c p) -> p c", p=P))
+        for b in range(H_PASSES):
+            for a in range(1, K_PASSES):
+                raw = sb("w1_raw%d_%d" % (a, b), [P, PACK, PASS], F32)
+                nc.sync.dma_start(raw[:], w1_rows(a)[:, :, b * PASS : (b + 1) * PASS])
+                w1_raw[a, b] = raw[:]
+        v2_win = [load_words("v2_win%d" % b, tab2_words[b]) for b in range(H_PASSES)]
+        v3_win = [load_words("v3_win%d" % b, tab3_words[b]) for b in range(H_PASSES)]
+
+        ident = sb("ident", [P, P], F32)
+        make_identity(nc, ident[:])
+
+        v_codes, v_scale = [], []
+        h2_ps = [[bank(TILES * b + jt, "h2_ps%d_%d" % (b, jt)) for jt in range(TILES)] for b in range(H_PASSES)]
+        for a in range(K_PASSES):
+            v_codes.append(gather("v_codes%d" % a, U32, v_win[a][:], idx))
+            v_scale.append(gather("v_scale%d" % a, U8, v_scale_win[:, a * T : (a + 1) * T], idx))
+            for b in range(H_PASSES):
+                for jt in range(TILES):
+                    cols = slice(jt * P, (jt + 1) * P)
+                    nc.tensor.matmul_mx(
+                        out=h2_ps[b][jt][:],
+                        lhsT=v_codes[a][:, cols].bitcast(FP8X4),
+                        lhsT_scale=v_scale[a][:, cols],
+                        rhs=w4_codes[:, a, 2 * b * PASS : 2 * (b + 1) * PASS].bitcast(FP4X4),
+                        rhs_scale=w4_scale[:, a * H + b * PASS : a * H + (b + 1) * PASS],
+                        start=(a == 0),
+                        stop=(a == K_PASSES - 1),
+                    )
+
+        def by_word(ps):
+            return ps[:].rearrange("j (p u e) -> j u p e", u=2, e=2)
+
+        h2 = {}
+        for b in range(H_PASSES):
+            for jt in range(TILES):
+                h2[b, jt] = sb("h2_%d_%d" % (b, jt), [P, 2, P, 2], F32)
+                nc.scalar.copy(h2[b, jt][:], by_word(h2_ps[b][jt]))
+
+        h1_ps = [[bank(TILES * b + jt, "h1_ps%d_%d" % (b, jt)) for jt in range(TILES)] for b in range(H_PASSES)]
+
+        def round_w1(a, b, on_vector):
+            grouped = ring("w1_bf", 3, "w1_bf%d_%d" % (a, b), [P, PASS, PACK], BF16)
+            dst = grouped[:].rearrange("p (c n) i -> p c i n", n=4)
+            src = w1_raw[a, b].rearrange("p i (c n) -> p c i n", n=4)
+            if on_vector:
+                nc.vector.tensor_copy(dst, src)
+            else:
+                nc.scalar.copy(dst, src)
+            return grouped
+
+        def quantise_w1_and_multiply(a, b, grouped):
+            codes = sb("w1_codes%d_%d" % (a, b), [P, PASS], U32)
+            scale = sb("w1_scale%d_%d" % (a, b), [P, PASS], U8)
+            nc.vector.quantize_mx(
+                out=codes[:].bitcast(FP8X4), scales=scale[:], in_=grouped[:].rearrange("p c i -> p (c i)")
+            )
+            for jt in range(TILES):
+                cols = slice(jt * P, (jt + 1) * P)
+                nc.tensor.matmul_mx(
+                    out=h1_ps[b][jt][:],
+                    lhsT=v_codes[a][:, cols].bitcast(FP8X4),
+                    lhsT_scale=v_scale[a][:, cols],
+                    rhs=codes[:].bitcast(FP8X4),
+                    rhs_scale=scale[:],
+                    start=(a == 0),
+                    stop=(a == K_PASSES - 1),
+                )
+
+        v2_scale = gather("v2_scale", U8, v2_scale_win[:], idx2)
+        rounded = [round_w1(0, b, on_vector=True) for b in range(H_PASSES)]
+        for b in range(H_PASSES):
+            quantise_w1_and_multiply(0, b, rounded[b])
+        v3_scale = gather("v3_scale", U8, v3_scale_win[:], idx3)
+
+        h_codes = [sb("h_codes%d" % b, [P, S], U32) for b in range(H_PASSES)]
+        h_scale = [sb("h_scale%d" % b, [P, S], U8) for b in range(H_PASSES)]
+        turn_banks = [[0, 1], [2, 3]]
+        for b in range(H_PASSES):
+            for a in range(1, K_PASSES):
+                quantise_w1_and_multiply(a, b, round_w1(a, b, on_vector=(a == 1 and b == 0)))
+            for jh in range(2):
+                turned = bank(turn_banks[b][jh], "turned%d_%d" % (b, jh))
+                turned_v = turned[:].rearrange("p (t u j) -> p t u j", t=2, u=2)
+                hb = []
+                for t in range(2):
+                    jt = 2 * jh + t
+                    h_bf = ring("h_bf", 4, "h_bf%d_%d" % (b, jt), [P, 2, P, 2], BF16)
+                    nc.vector.tensor_tensor(h_bf[:], by_word(h1_ps[b][jt]), h2[b, jt][:], ALU.max)
+                    hb.append(h_bf)
+                for t in range(2):
+                    words = hb[t][:].rearrange("j u p e -> j (u p e)").bitcast(F32)
+                    for u in range(2):
+                        nc.tensor.transpose(turned_v[:, t, u, :], words[:, u * P : (u + 1) * P], ident[:])
+                h_grouped = sb("h_grouped%d_%d" % (b, jh), [P, HALF * PACK], BF16)
+                nc.scalar.copy(
+                    h_grouped[:].bitcast(F32).rearrange("p (t j u) -> p t j u", t=2, u=2),
+                    turned[:].rearrange("p (t u j) -> p t j u", t=2, u=2),
+                )
+                cols = slice(jh * HALF, (jh + 1) * HALF)
+                nc.vector.quantize_mx(
+                    out=h_codes[b][:, cols].bitcast(FP8X4), scales=h_scale[b][:, cols], in_=h_grouped[:]
+                )
+        v2_codes = [gather("v2_codes%d" % b, U32, v2_win[b][:], idx2) for b in range(H_PASSES)]
+
+        room = sb("room", [P, TILES, S], F32)
+        room_banks = [[0, 1], [4, 5]]
+        for jh in range(2):
+            cols = slice(jh * HALF, (jh + 1) * HALF)
+            for mp in range(2):
+                e2 = bank(room_banks[jh][mp], "e2_%d_%d" % (jh, mp))
+                for t in range(2):
+                    mcols = slice((2 * mp + t) * P, (2 * mp + t + 1) * P)
+                    for b in range(H_PASSES):
+                        nc.tensor.matmul_mx(
+                            out=e2[:, t * HALF : (t + 1) * HALF],
+                            lhsT=v2_codes[b][:, mcols].bitcast(FP8X4),
+                            lhsT_scale=v2_scale[4 * b : P, mcols],
+                            rhs=h_codes[b][:, cols].bitcast(FP8X4),
+                            rhs_scale=h_scale[b][:, cols],
+                            start=(b == 0),
+                            stop=(b == H_PASSES - 1),
+                        )
+                nc.scalar.activation(
+                    room[:, 2 * mp : 2 * mp + 2, cols], e2[:].rearrange("m (t j) -> m t j", t=2), ACT.Silu
+                )
+
+        mate_banks = [6, 7, 2, 3]
+        e3 = [bank(mate_banks[mt], "e3_%d" % mt) for mt in range(TILES)]
+        for b in range(H_PASSES):
+            codes = sb("v3_codes%d" % b, [P, S], U32)
+            pieces = 1 + b
+            for mt in range(TILES):
+                if mt % (TILES // pieces) == 0:
+                    n = S // pieces
+                    lo = mt * P
+                    nc.vector.tensor_copy(
+                        codes[:, lo : lo + n], v3_win[b][:].indirect(idx3[:, lo // 16 : (lo + n) // 16])
+                    )
+                mcols = slice(mt * P, (mt + 1) * P)
+                nc.tensor.matmul_mx(
+                    out=e3[mt][:],
+                    lhsT=codes[:, mcols].bitcast(FP8X4),
+                    lhsT_scale=v3_scale[4 * b : P, mcols],
+                    rhs=h_codes[b][:].bitcast(FP8X4),
+                    rhs_scale=h_scale[b][:],
+                    start=(b == 0),
+                    stop=(b == H_PASSES - 1),
+                )
+        for mt in range(TILES):
+            mate = ring("mate", 2, "mate%d" % mt, [P, S], F32)
+            nc.scalar.activation(mate[:], e3[mt][:], ACT.Tanh, scale=steep_sb[:, mt : mt + 1])
+            score = sb("score%d" % mt, [P, S], F32)
+            nc.vector.tensor_tensor(score[:], mate[:], room[:, mt, :], ALU.add)
+            nc.sync.dma_start(out[mt * P : (mt + 1) * P, :], score[:])

@@ -25,6 +25,9 @@ H_PASSES = H // PASS
 TILES = S // P
 QUADS = 4
 HALF = S // 2
+V_ROW = 16
+OFFER_ROW = 64
+OFFER_PLANE = 4
 
 
 def tile_list_flatshare_pair_ranking_kernel(
@@ -36,8 +39,8 @@ def tile_list_flatshare_pair_ranking_kernel(
         keep = ctx.enter_context(tc.tile_pool(name="keep", bufs=1))
         psum = ctx.enter_context(tc.psum_pool(name="psum", bufs=1))
 
-        def sb(name, shape, dtype):
-            return keep.tile(shape, dtype, name=name, align_bytes=64)
+        def sb(name, shape, dtype, tag=None):
+            return keep.tile(shape, dtype, name=name, tag=tag or name, align_bytes=64)
 
         def ring(tag, bufs, name, shape, dtype):
             return keep.tile(shape, dtype, name=name, tag=tag, bufs=bufs, align_bytes=64)
@@ -62,75 +65,85 @@ def tile_list_flatshare_pair_ranking_kernel(
                     scales.bitcast(I32)[:, 4 * q : 4 * q + 4, :].rearrange("a r t -> r a t"),
                 )
 
-        def load_planes_stacked(plane, scales, passes):
+        def load_scale_rows(name, scales, passes, first):
+            rows = 16 * passes
+            win = sb(name, [P, T], U8)
+            words = win[:].bitcast(I32)
+            nc.gpsimd.memset(words[0:first, :], 0)
+            nc.gpsimd.memset(words[first + rows : P, :], 0)
+            nc.sync.dma_start(words[first : first + rows, :], scales.bitcast(I32).rearrange("a q t -> q a t"))
+            return win
+
+        def deal_scale_rows(queue, plane, plane_row, picked, passes, first):
+            rows = 4 * passes
             for q in range(QUADS):
-                nc.sync.dma_start(
-                    plane[32 * q : 32 * q + 4 * passes, :].bitcast(I32),
-                    scales.bitcast(I32)[:, 4 * q : 4 * q + 4, :],
+                queue.dma_start(
+                    plane[32 * q + plane_row : 32 * q + plane_row + 4, :].bitcast(I32),
+                    picked[first + rows * q : first + rows * (q + 1), :].bitcast(I32),
                 )
 
-        def gather(name, dtype, window, offsets):
-            picked = sb(name, [P, S], dtype)
+        def gather(name, dtype, window, offsets, tag=None):
+            picked = sb(name, [P, S], dtype, tag)
             nc.vector.tensor_copy(picked[:], window.indirect(offsets[:]))
             return picked
 
-        v_scale_win = sb("v_scale_win", [P, K_PASSES * T], U8)
         w4_scale = sb("w4_scale", [P, K_PASSES * H], U8)
-        v2_scale_win = sb("v2_scale_win", [P, T], U8)
-        v3_scale_win = sb("v3_scale_win", [P, T], U8)
-        nc.vector.memset(v_scale_win[:].bitcast(I32), 0)
+        v_scale = sb("v_scale", [P, K_PASSES * S], U8)
+        offer_scale = sb("offer_scale", [P, H_PASSES * 2 * S], U8)
         nc.vector.memset(w4_scale[:].bitcast(I32), 0)
-        nc.gpsimd.memset(v2_scale_win[:].bitcast(I32), 0)
-        nc.gpsimd.memset(v3_scale_win[:].bitcast(I32), 0)
+        nc.vector.memset(v_scale[:].bitcast(I32), 0)
+        nc.vector.memset(offer_scale[:].bitcast(I32), 0)
 
         idx = load_list("idx", offs)
+        v_scale_win = load_scale_rows("v_scale_win", tab_scales, K_PASSES, V_ROW)
+        v_scale_rows = gather("v_scale_rows", U8, v_scale_win[:], idx)
+        deal_scale_rows(nc.scalar, v_scale, 0, v_scale_rows, K_PASSES, V_ROW)
         v_win = [load_words("v_win0", tab_words[0])]
-        load_planes_side_by_side(v_scale_win, tab_scales, K_PASSES)
+        load_planes_side_by_side(w4_scale, w4_scales, K_PASSES)
+        idx2 = load_list("idx2", offs2)
+        v2_scale_win = load_scale_rows("v2_scale_win", tab2_scales, H_PASSES, OFFER_ROW)
         w4_codes = sb("w4_codes", [P, K_PASSES, 2 * H], U8)
         nc.sync.dma_start(w4_codes[:].bitcast(I32), w4_words.bitcast(I32).rearrange("a p c -> p a c"))
-        load_planes_side_by_side(w4_scale, w4_scales, K_PASSES)
         v_win.append(load_words("v_win1", tab_words[1]))
         v_win.append(load_words("v_win2", tab_words[2]))
-        idx2 = load_list("idx2", offs2)
-        load_planes_stacked(v2_scale_win, tab2_scales, H_PASSES)
+        idx3 = load_list("idx3", offs3)
+        v3_scale_win = load_scale_rows("v3_scale_win", tab3_scales, H_PASSES, OFFER_ROW)
 
         w1_raw = {}
 
         def w1_rows(a):
             return w1[a * PASS : (a + 1) * PASS, :].rearrange("(p i) c -> p i c", i=PACK)
 
-        raw = sb("w1_raw0", [P, PACK, H], F32)
-        nc.sync.dma_start(raw[:], w1_rows(0))
+        def load_w1(a, b):
+            raw = sb("w1_raw%d_%d" % (a, b), [P, PACK, PASS], F32)
+            nc.sync.dma_start(raw[:], w1_rows(a)[:, :, b * PASS : (b + 1) * PASS])
+            w1_raw[a, b] = raw[:]
+
+        load_w1(0, 0)
+        steep_rows = sb("steep_rows", [P, P], F32)
+        nc.gpsimd.memset(steep_rows[:], 0.0)
+        nc.sync.dma_start(steep_rows[0:TILES, :], steep.rearrange("(c p) -> c p", p=P))
         for b in range(H_PASSES):
-            w1_raw[0, b] = raw[:, :, b * PASS : (b + 1) * PASS]
-        idx3 = load_list("idx3", offs3)
-        load_planes_stacked(v3_scale_win, tab3_scales, H_PASSES)
-        steep_sb = keep.tile([P, TILES], F32, name="steep_sb")
-        with nc.allow_non_contiguous_dma(reason="one factor for each output row"):
-            nc.sync.dma_start(steep_sb[:], steep.rearrange("(c p) -> p c", p=P))
-        for b in range(H_PASSES):
-            for a in range(1, K_PASSES):
-                raw = sb("w1_raw%d_%d" % (a, b), [P, PACK, PASS], F32)
-                nc.sync.dma_start(raw[:], w1_rows(a)[:, :, b * PASS : (b + 1) * PASS])
-                w1_raw[a, b] = raw[:]
+            for a in range(K_PASSES):
+                if (a, b) != (0, 0):
+                    load_w1(a, b)
         v2_win = [load_words("v2_win%d" % b, tab2_words[b]) for b in range(H_PASSES)]
         v3_win = [load_words("v3_win%d" % b, tab3_words[b]) for b in range(H_PASSES)]
 
         ident = sb("ident", [P, P], F32)
         make_identity(nc, ident[:])
 
-        v_codes, v_scale = [], []
+        v_codes = []
         h2_ps = [[bank(TILES * b + jt, "h2_ps%d_%d" % (b, jt)) for jt in range(TILES)] for b in range(H_PASSES)]
         for a in range(K_PASSES):
             v_codes.append(gather("v_codes%d" % a, U32, v_win[a][:], idx))
-            v_scale.append(gather("v_scale%d" % a, U8, v_scale_win[:, a * T : (a + 1) * T], idx))
             for b in range(H_PASSES):
                 for jt in range(TILES):
                     cols = slice(jt * P, (jt + 1) * P)
                     nc.tensor.matmul_mx(
                         out=h2_ps[b][jt][:],
                         lhsT=v_codes[a][:, cols].bitcast(FP8X4),
-                        lhsT_scale=v_scale[a][:, cols],
+                        lhsT_scale=v_scale[:, a * S + jt * P : a * S + (jt + 1) * P],
                         rhs=w4_codes[:, a, 2 * b * PASS : 2 * (b + 1) * PASS].bitcast(FP4X4),
                         rhs_scale=w4_scale[:, a * H + b * PASS : a * H + (b + 1) * PASS],
                         start=(a == 0),
@@ -148,46 +161,64 @@ def tile_list_flatshare_pair_ranking_kernel(
 
         h1_ps = [[bank(TILES * b + jt, "h1_ps%d_%d" % (b, jt)) for jt in range(TILES)] for b in range(H_PASSES)]
 
-        def round_w1(a, b, on_vector):
-            grouped = ring("w1_bf", 3, "w1_bf%d_%d" % (a, b), [P, PASS, PACK], BF16)
-            dst = grouped[:].rearrange("p (c n) i -> p c i n", n=4)
-            src = w1_raw[a, b].rearrange("p i (c n) -> p c i n", n=4)
-            if on_vector:
-                nc.vector.tensor_copy(dst, src)
-            else:
-                nc.scalar.copy(dst, src)
-            return grouped
+        def round_w1(a, b, engines):
+            width = PASS // len(engines)
+            pieces = []
+            for k, copy in enumerate(engines):
+                name = "w1_bf%d_%d_%d" % (a, b, k)
+                if len(engines) == 1:
+                    grouped = ring("w1_bf", 3, name, [P, width, PACK], BF16)
+                else:
+                    grouped = sb(name, [P, width, PACK], BF16)
+                copy(
+                    grouped[:].rearrange("p (c n) i -> p c i n", n=2),
+                    w1_raw[a, b][:, :, k * width : (k + 1) * width].rearrange("p i (c n) -> p c i n", n=2),
+                )
+                pieces.append(grouped)
+            return pieces
 
-        def quantise_w1_and_multiply(a, b, grouped):
+        def quantise_w1_and_multiply(a, b, pieces):
             codes = sb("w1_codes%d_%d" % (a, b), [P, PASS], U32)
             scale = sb("w1_scale%d_%d" % (a, b), [P, PASS], U8)
-            nc.vector.quantize_mx(
-                out=codes[:].bitcast(FP8X4), scales=scale[:], in_=grouped[:].rearrange("p c i -> p (c i)")
-            )
+            width = PASS // len(pieces)
+            for k, grouped in enumerate(pieces):
+                part = slice(k * width, (k + 1) * width)
+                nc.vector.quantize_mx(
+                    out=codes[:, part].bitcast(FP8X4),
+                    scales=scale[:, part],
+                    in_=grouped[:].rearrange("p c i -> p (c i)"),
+                )
             for jt in range(TILES):
                 cols = slice(jt * P, (jt + 1) * P)
                 nc.tensor.matmul_mx(
                     out=h1_ps[b][jt][:],
                     lhsT=v_codes[a][:, cols].bitcast(FP8X4),
-                    lhsT_scale=v_scale[a][:, cols],
+                    lhsT_scale=v_scale[:, a * S + jt * P : a * S + (jt + 1) * P],
                     rhs=codes[:].bitcast(FP8X4),
                     rhs_scale=scale[:],
                     start=(a == 0),
                     stop=(a == K_PASSES - 1),
                 )
 
-        v2_scale = gather("v2_scale", U8, v2_scale_win[:], idx2)
-        rounded = [round_w1(0, b, on_vector=True) for b in range(H_PASSES)]
-        for b in range(H_PASSES):
-            quantise_w1_and_multiply(0, b, rounded[b])
-        v3_scale = gather("v3_scale", U8, v3_scale_win[:], idx3)
+        offer_scale_rows = sb("offer_scale_rows", [P, 2 * S], U8)
+        nc.vector.tensor_copy(offer_scale_rows[:, 0:S], v2_scale_win[:].indirect(idx2[:]))
+        nc.vector.tensor_copy(offer_scale_rows[:, S : 2 * S], v3_scale_win[:].indirect(idx3[:]))
+        deal_scale_rows(nc.gpsimd, offer_scale, OFFER_PLANE, offer_scale_rows, H_PASSES, OFFER_ROW)
+
+        def offer_plane(b, table, mt):
+            lo = (2 * b + table) * S + mt * P
+            return offer_scale[OFFER_PLANE:P, lo : lo + P]
 
         h_codes = [sb("h_codes%d" % b, [P, S], U32) for b in range(H_PASSES)]
         h_scale = [sb("h_scale%d" % b, [P, S], U8) for b in range(H_PASSES)]
         turn_banks = [[0, 1], [2, 3]]
         for b in range(H_PASSES):
-            for a in range(1, K_PASSES):
-                quantise_w1_and_multiply(a, b, round_w1(a, b, on_vector=(a == 1 and b == 0)))
+            for a in range(K_PASSES):
+                if a == K_PASSES - 1:
+                    engines = [nc.vector.tensor_copy, nc.scalar.copy]
+                else:
+                    engines = [nc.vector.tensor_copy] if b == 0 else [nc.scalar.copy]
+                quantise_w1_and_multiply(a, b, round_w1(a, b, engines))
             for jh in range(2):
                 turned = bank(turn_banks[b][jh], "turned%d_%d" % (b, jh))
                 turned_v = turned[:].rearrange("p (t u j) -> p t u j", t=2, u=2)
@@ -206,59 +237,67 @@ def tile_list_flatshare_pair_ranking_kernel(
                     h_grouped[:].bitcast(F32).rearrange("p (t j u) -> p t j u", t=2, u=2),
                     turned[:].rearrange("p (t u j) -> p t j u", t=2, u=2),
                 )
+                if (b, jh) == (0, 1):
+                    steep_ps = bank(3, "steep_ps")
+                    nc.tensor.transpose(steep_ps[:, 0:P], steep_rows[:], ident[:])
+                    steep_sb = sb("steep_sb", [P, TILES], F32)
+                    nc.scalar.copy(steep_sb[:], steep_ps[:, 0:TILES])
                 cols = slice(jh * HALF, (jh + 1) * HALF)
                 nc.vector.quantize_mx(
                     out=h_codes[b][:, cols].bitcast(FP8X4), scales=h_scale[b][:, cols], in_=h_grouped[:]
                 )
-        v2_codes = [gather("v2_codes%d" % b, U32, v2_win[b][:], idx2) for b in range(H_PASSES)]
+        v2_codes = [
+            gather("v2_codes0", U32, v2_win[0][:], idx2, "w1_bf2_1_1"),
+            gather("v2_codes1", U32, v2_win[1][:], idx2, "h_grouped1_0"),
+        ]
 
         room = sb("room", [P, TILES, S], F32)
         room_banks = [[0, 1], [4, 5]]
-        for jh in range(2):
-            cols = slice(jh * HALF, (jh + 1) * HALF)
-            for mp in range(2):
-                e2 = bank(room_banks[jh][mp], "e2_%d_%d" % (jh, mp))
-                for t in range(2):
-                    mcols = slice((2 * mp + t) * P, (2 * mp + t + 1) * P)
-                    for b in range(H_PASSES):
+        e2 = [[bank(room_banks[jh][mp], "e2_%d_%d" % (jh, mp)) for mp in range(2)] for jh in range(2)]
+        for b in range(H_PASSES):
+            for jh in range(2):
+                cols = slice(jh * HALF, (jh + 1) * HALF)
+                for mp in range(2):
+                    for t in range(2):
+                        mcols = slice((2 * mp + t) * P, (2 * mp + t + 1) * P)
                         nc.tensor.matmul_mx(
-                            out=e2[:, t * HALF : (t + 1) * HALF],
+                            out=e2[jh][mp][:, t * HALF : (t + 1) * HALF],
                             lhsT=v2_codes[b][:, mcols].bitcast(FP8X4),
-                            lhsT_scale=v2_scale[4 * b : P, mcols],
+                            lhsT_scale=offer_plane(b, 0, 2 * mp + t),
                             rhs=h_codes[b][:, cols].bitcast(FP8X4),
                             rhs_scale=h_scale[b][:, cols],
-                            start=(b == 0),
-                            stop=(b == H_PASSES - 1),
+                            start=(b == 0 and t == 0),
+                            stop=(b == H_PASSES - 1 and t == 1),
                         )
-                nc.scalar.activation(
-                    room[:, 2 * mp : 2 * mp + 2, cols], e2[:].rearrange("m (t j) -> m t j", t=2), ACT.Silu
-                )
+                    if b == H_PASSES - 1:
+                        nc.scalar.activation(
+                            room[:, 2 * mp : 2 * mp + 2, cols],
+                            e2[jh][mp][:].rearrange("m (t j) -> m t j", t=2),
+                            ACT.Silu,
+                        )
 
         mate_banks = [6, 7, 2, 3]
         e3 = [bank(mate_banks[mt], "e3_%d" % mt) for mt in range(TILES)]
-        for b in range(H_PASSES):
-            codes = sb("v3_codes%d" % b, [P, S], U32)
-            pieces = 1 + b
-            for mt in range(TILES):
-                if mt % (TILES // pieces) == 0:
-                    n = S // pieces
-                    lo = mt * P
-                    nc.vector.tensor_copy(
-                        codes[:, lo : lo + n], v3_win[b][:].indirect(idx3[:, lo // 16 : (lo + n) // 16])
-                    )
-                mcols = slice(mt * P, (mt + 1) * P)
-                nc.tensor.matmul_mx(
-                    out=e3[mt][:],
-                    lhsT=codes[:, mcols].bitcast(FP8X4),
-                    lhsT_scale=v3_scale[4 * b : P, mcols],
-                    rhs=h_codes[b][:].bitcast(FP8X4),
-                    rhs_scale=h_scale[b][:],
-                    start=(b == 0),
-                    stop=(b == H_PASSES - 1),
+        v3_codes = sb("v3_codes", [P, H_PASSES * S], U32, "h_grouped1_1")
+        for mh in range(2):
+            for b in range(H_PASSES):
+                lo = mh * HALF
+                nc.vector.tensor_copy(
+                    v3_codes[:, b * S + lo : b * S + lo + HALF],
+                    v3_win[b][:].indirect(idx3[:, lo // 16 : (lo + HALF) // 16]),
                 )
+                for mt in range(2 * mh, 2 * mh + 2):
+                    nc.tensor.matmul_mx(
+                        out=e3[mt][:],
+                        lhsT=v3_codes[:, b * S + mt * P : b * S + (mt + 1) * P].bitcast(FP8X4),
+                        lhsT_scale=offer_plane(b, 1, mt),
+                        rhs=h_codes[b][:].bitcast(FP8X4),
+                        rhs_scale=h_scale[b][:],
+                        start=(b == 0),
+                        stop=(b == H_PASSES - 1),
+                    )
         for mt in range(TILES):
-            mate = ring("mate", 2, "mate%d" % mt, [P, S], F32)
-            nc.scalar.activation(mate[:], e3[mt][:], ACT.Tanh, scale=steep_sb[:, mt : mt + 1])
             score = sb("score%d" % mt, [P, S], F32)
-            nc.vector.tensor_tensor(score[:], mate[:], room[:, mt, :], ALU.add)
+            nc.scalar.activation(score[:], e3[mt][:], ACT.Tanh, scale=steep_sb[:, mt : mt + 1])
+            nc.vector.tensor_tensor(score[:], score[:], room[:, mt, :], ALU.add)
             nc.sync.dma_start(out[mt * P : (mt + 1) * P, :], score[:])

@@ -53,16 +53,16 @@ def tile_list_flatshare_pair_ranking_kernel(
             nc.sync.dma_start(lst[:], src)
             return lst
 
-        def load_words(name, words):
-            win = sb(name, [P, T], U32)
+        def load_words(name, words, tag=None):
+            win = sb(name, [P, T], U32, tag)
             nc.sync.dma_start(win[:].bitcast(I32), words.rearrange("p t i -> p (t i)").bitcast(I32))
             return win
 
         def load_planes_side_by_side(plane, scales, passes):
-            for q in range(QUADS):
+            for r in range(4):
                 nc.sync.dma_start(
-                    plane[32 * q : 32 * q + 4, :].bitcast(I32).rearrange("r (a t) -> r a t", a=passes),
-                    scales.bitcast(I32)[:, 4 * q : 4 * q + 4, :].rearrange("a r t -> r a t"),
+                    plane[r:P:32, :].bitcast(I32).rearrange("q (a t) -> q a t", a=passes),
+                    scales.bitcast(I32)[:, r:16:4, :].rearrange("a q t -> q a t"),
                 )
 
         def load_scale_rows(name, scales, passes, first):
@@ -88,26 +88,22 @@ def tile_list_flatshare_pair_ranking_kernel(
             return picked
 
         w4_scale = sb("w4_scale", [P, K_PASSES * H], U8)
-        v_scale = sb("v_scale", [P, K_PASSES * S], U8)
+        v_scale_win = sb("v_scale_win", [P, K_PASSES * T], U8)
         offer_scale = sb("offer_scale", [P, H_PASSES * 2 * S], U8)
+        nc.vector.memset(v_scale_win[:].bitcast(I32), 0)
         nc.vector.memset(w4_scale[:].bitcast(I32), 0)
-        nc.vector.memset(v_scale[:].bitcast(I32), 0)
         nc.vector.memset(offer_scale[:].bitcast(I32), 0)
 
         idx = load_list("idx", offs)
-        v_scale_win = load_scale_rows("v_scale_win", tab_scales, K_PASSES, V_ROW)
-        v_scale_rows = gather("v_scale_rows", U8, v_scale_win[:], idx)
-        deal_scale_rows(nc.scalar, v_scale, 0, v_scale_rows, K_PASSES, V_ROW)
         v_win = [load_words("v_win0", tab_words[0])]
-        load_planes_side_by_side(w4_scale, w4_scales, K_PASSES)
-        idx2 = load_list("idx2", offs2)
-        v2_scale_win = load_scale_rows("v2_scale_win", tab2_scales, H_PASSES, OFFER_ROW)
+        load_planes_side_by_side(v_scale_win, tab_scales, K_PASSES)
         w4_codes = sb("w4_codes", [P, K_PASSES, 2 * H], U8)
         nc.sync.dma_start(w4_codes[:].bitcast(I32), w4_words.bitcast(I32).rearrange("a p c -> p a c"))
+        load_planes_side_by_side(w4_scale, w4_scales, K_PASSES)
         v_win.append(load_words("v_win1", tab_words[1]))
         v_win.append(load_words("v_win2", tab_words[2]))
-        idx3 = load_list("idx3", offs3)
-        v3_scale_win = load_scale_rows("v3_scale_win", tab3_scales, H_PASSES, OFFER_ROW)
+        idx2 = load_list("idx2", offs2)
+        v2_scale_win = load_scale_rows("v2_scale_win", tab2_scales, H_PASSES, OFFER_ROW)
 
         w1_raw = {}
 
@@ -120,6 +116,8 @@ def tile_list_flatshare_pair_ranking_kernel(
             w1_raw[a, b] = raw[:]
 
         load_w1(0, 0)
+        idx3 = load_list("idx3", offs3)
+        v3_scale_win = load_scale_rows("v3_scale_win", tab3_scales, H_PASSES, OFFER_ROW)
         steep_rows = sb("steep_rows", [P, P], F32)
         nc.gpsimd.memset(steep_rows[:], 0.0)
         nc.sync.dma_start(steep_rows[0:TILES, :], steep.rearrange("(c p) -> c p", p=P))
@@ -127,28 +125,38 @@ def tile_list_flatshare_pair_ranking_kernel(
             for a in range(K_PASSES):
                 if (a, b) != (0, 0):
                     load_w1(a, b)
-        v2_win = [load_words("v2_win%d" % b, tab2_words[b]) for b in range(H_PASSES)]
-        v3_win = [load_words("v3_win%d" % b, tab3_words[b]) for b in range(H_PASSES)]
 
         ident = sb("ident", [P, P], F32)
         make_identity(nc, ident[:])
 
-        v_codes = []
-        h2_ps = [[bank(TILES * b + jt, "h2_ps%d_%d" % (b, jt)) for jt in range(TILES)] for b in range(H_PASSES)]
+        v_codes, v_scale = [], []
         for a in range(K_PASSES):
             v_codes.append(gather("v_codes%d" % a, U32, v_win[a][:], idx))
+            v_scale.append(gather("v_scale%d" % a, U8, v_scale_win[:, a * T : (a + 1) * T], idx))
+        offer_scale_rows = sb("offer_scale_rows", [P, 2 * S], U8)
+        nc.vector.tensor_copy(offer_scale_rows[:, 0:S], v2_scale_win[:].indirect(idx2[:]))
+        nc.vector.tensor_copy(offer_scale_rows[:, S : 2 * S], v3_scale_win[:].indirect(idx3[:]))
+        deal_scale_rows(nc.sync, offer_scale, OFFER_PLANE, offer_scale_rows, H_PASSES, OFFER_ROW)
+        v2_win = [
+            load_words("v2_win0", tab2_words[0], "v2_scale_win"),
+            load_words("v2_win1", tab2_words[1], "v3_scale_win"),
+        ]
+        h2_ps = [[bank(TILES * b + jt, "h2_ps%d_%d" % (b, jt)) for jt in range(TILES)] for b in range(H_PASSES)]
+        for a in range(K_PASSES):
             for b in range(H_PASSES):
                 for jt in range(TILES):
                     cols = slice(jt * P, (jt + 1) * P)
                     nc.tensor.matmul_mx(
                         out=h2_ps[b][jt][:],
                         lhsT=v_codes[a][:, cols].bitcast(FP8X4),
-                        lhsT_scale=v_scale[:, a * S + jt * P : a * S + (jt + 1) * P],
+                        lhsT_scale=v_scale[a][:, cols],
                         rhs=w4_codes[:, a, 2 * b * PASS : 2 * (b + 1) * PASS].bitcast(FP4X4),
                         rhs_scale=w4_scale[:, a * H + b * PASS : a * H + (b + 1) * PASS],
                         start=(a == 0),
                         stop=(a == K_PASSES - 1),
                     )
+
+        v3_win = [load_words("v3_win0", tab3_words[0], "w4_codes")]
 
         def by_word(ps):
             return ps[:].rearrange("j (p u e) -> j u p e", u=2, e=2)
@@ -193,17 +201,13 @@ def tile_list_flatshare_pair_ranking_kernel(
                 nc.tensor.matmul_mx(
                     out=h1_ps[b][jt][:],
                     lhsT=v_codes[a][:, cols].bitcast(FP8X4),
-                    lhsT_scale=v_scale[:, a * S + jt * P : a * S + (jt + 1) * P],
+                    lhsT_scale=v_scale[a][:, cols],
                     rhs=codes[:].bitcast(FP8X4),
                     rhs_scale=scale[:],
                     start=(a == 0),
                     stop=(a == K_PASSES - 1),
                 )
 
-        offer_scale_rows = sb("offer_scale_rows", [P, 2 * S], U8)
-        nc.vector.tensor_copy(offer_scale_rows[:, 0:S], v2_scale_win[:].indirect(idx2[:]))
-        nc.vector.tensor_copy(offer_scale_rows[:, S : 2 * S], v3_scale_win[:].indirect(idx3[:]))
-        deal_scale_rows(nc.gpsimd, offer_scale, OFFER_PLANE, offer_scale_rows, H_PASSES, OFFER_ROW)
 
         def offer_plane(b, table, mt):
             lo = (2 * b + table) * S + mt * P
@@ -219,13 +223,19 @@ def tile_list_flatshare_pair_ranking_kernel(
                 else:
                     engines = [nc.vector.tensor_copy] if b == 0 else [nc.scalar.copy]
                 quantise_w1_and_multiply(a, b, round_w1(a, b, engines))
+                if (a, b) == (1, 0):
+                    v3_win.append(load_words("v3_win1", tab3_words[1], "w1_raw1_0"))
             for jh in range(2):
                 turned = bank(turn_banks[b][jh], "turned%d_%d" % (b, jh))
                 turned_v = turned[:].rearrange("p (t u j) -> p t u j", t=2, u=2)
                 hb = []
                 for t in range(2):
                     jt = 2 * jh + t
-                    h_bf = ring("h_bf", 4, "h_bf%d_%d" % (b, jt), [P, 2, P, 2], BF16)
+                    if (b, jt) == (1, 2):
+                        v2_codes = [gather("v2_codes0", U32, v2_win[0][:], idx2, "w1_bf2_1_1")]
+                        h_bf = sb("h_bf1_2", [P, 2, P, 2], BF16, "v2_scale_win")
+                    else:
+                        h_bf = ring("h_bf", 4, "h_bf%d_%d" % (b, jt), [P, 2, P, 2], BF16)
                     nc.vector.tensor_tensor(h_bf[:], by_word(h1_ps[b][jt]), h2[b, jt][:], ALU.max)
                     hb.append(h_bf)
                 for t in range(2):
@@ -246,10 +256,7 @@ def tile_list_flatshare_pair_ranking_kernel(
                 nc.vector.quantize_mx(
                     out=h_codes[b][:, cols].bitcast(FP8X4), scales=h_scale[b][:, cols], in_=h_grouped[:]
                 )
-        v2_codes = [
-            gather("v2_codes0", U32, v2_win[0][:], idx2, "w1_bf2_1_1"),
-            gather("v2_codes1", U32, v2_win[1][:], idx2, "h_grouped1_0"),
-        ]
+        v2_codes.append(gather("v2_codes1", U32, v2_win[1][:], idx2, "h_grouped1_0"))
 
         room = sb("room", [P, TILES, S], F32)
         room_banks = [[0, 1], [4, 5]]

@@ -133,14 +133,12 @@ def tile_list_flatshare_pair_ranking_kernel(
         for a in range(K_PASSES):
             v_codes.append(gather("v_codes%d" % a, U32, v_win[a][:], idx))
             v_scale.append(gather("v_scale%d" % a, U8, v_scale_win[:, a * T : (a + 1) * T], idx))
+        v2_win = [load_words("v2_win%d" % b, tab2_words[b]) for b in range(H_PASSES)]
         offer_scale_rows = sb("offer_scale_rows", [P, 2 * S], U8)
         nc.vector.tensor_copy(offer_scale_rows[:, 0:S], v2_scale_win[:].indirect(idx2[:]))
         nc.vector.tensor_copy(offer_scale_rows[:, S : 2 * S], v3_scale_win[:].indirect(idx3[:]))
         deal_scale_rows(nc.sync, offer_scale, OFFER_PLANE, offer_scale_rows, H_PASSES, OFFER_ROW)
-        v2_win = [
-            load_words("v2_win0", tab2_words[0], "v2_scale_win"),
-            load_words("v2_win1", tab2_words[1], "v3_scale_win"),
-        ]
+        v3_win = [load_words("v3_win0", tab3_words[0], "v3_scale_win")]
         h2_ps = [[bank(TILES * b + jt, "h2_ps%d_%d" % (b, jt)) for jt in range(TILES)] for b in range(H_PASSES)]
         for a in range(K_PASSES):
             for b in range(H_PASSES):
@@ -155,8 +153,6 @@ def tile_list_flatshare_pair_ranking_kernel(
                         start=(a == 0),
                         stop=(a == K_PASSES - 1),
                     )
-
-        v3_win = [load_words("v3_win0", tab3_words[0], "w4_codes")]
 
         def by_word(ps):
             return ps[:].rearrange("j (p u e) -> j u p e", u=2, e=2)
@@ -223,8 +219,8 @@ def tile_list_flatshare_pair_ranking_kernel(
                 else:
                     engines = [nc.vector.tensor_copy] if b == 0 else [nc.scalar.copy]
                 quantise_w1_and_multiply(a, b, round_w1(a, b, engines))
-                if (a, b) == (1, 0):
-                    v3_win.append(load_words("v3_win1", tab3_words[1], "w1_raw1_0"))
+                if (a, b) == (2, 0):
+                    v3_win.append(load_words("v3_win1", tab3_words[1], "w1_raw2_0"))
             for jh in range(2):
                 turned = bank(turn_banks[b][jh], "turned%d_%d" % (b, jh))
                 turned_v = turned[:].rearrange("p (t u j) -> p t u j", t=2, u=2)
@@ -233,7 +229,7 @@ def tile_list_flatshare_pair_ranking_kernel(
                     jt = 2 * jh + t
                     if (b, jt) == (1, 2):
                         v2_codes = [gather("v2_codes0", U32, v2_win[0][:], idx2, "w1_bf2_1_1")]
-                        h_bf = sb("h_bf1_2", [P, 2, P, 2], BF16, "v2_scale_win")
+                        h_bf = sb("h_bf1_2", [P, 2, P, 2], BF16, "v2_win0")
                     else:
                         h_bf = ring("h_bf", 4, "h_bf%d_%d" % (b, jt), [P, 2, P, 2], BF16)
                     nc.vector.tensor_tensor(h_bf[:], by_word(h1_ps[b][jt]), h2[b, jt][:], ALU.max)

from contextlib import ExitStack

import concourse.mybir as mybir
from concourse.masks import make_identity

K, H, T, S = 1536, 1024, 2048, 512
FLOPS = 2 * (2 * K * H * S + 2 * H * S * S)

F32 = mybir.dt.float32
BF16 = mybir.dt.bfloat16
I32 = mybir.dt.int32
U32 = mybir.dt.uint32
U16 = mybir.dt.uint16
U8 = mybir.dt.uint8
FP8X4 = mybir.dt.float8_e4m3fn_x4
FP4X4 = mybir.dt.float4_e2m1fn_x4
ACT = mybir.ActivationFunctionType
ALU = mybir.AluOpType

P = 128
PACK = 4
PASS = P * PACK
K_PASSES = K // PASS
H_PASSES = H // PASS
TILES = S // P
QUADS = 4
HALF = S // 2
V_ROW = 16
OFFER_ROW = 64
OFFER_PLANE = 4


def tile_list_flatshare_pair_ranking_kernel(
    tc, tab_words, tab_scales, tab2_words, tab2_scales, tab3_words, tab3_scales,
    w1, w4_words, w4_scales, steep, offs, offs2, offs3, out,
):
    nc = tc.nc
    with ExitStack() as ctx:
        keep = ctx.enter_context(tc.tile_pool(name="keep", bufs=1))
        psum = ctx.enter_context(tc.psum_pool(name="psum", bufs=1))

        def sb(name, shape, dtype, tag=None):
            return keep.tile(shape, dtype, name=name, tag=tag or name, align_bytes=64)

        def ring(tag, bufs, name, shape, dtype):
            return keep.tile(shape, dtype, name=name, tag=tag, bufs=bufs, align_bytes=64)

        def bank(i, name):
            return psum.tile([P, PASS], F32, name=name, tag="bank%d" % i)

        def load_list(name, src):
            lst = keep.tile([P, S // 16], U16, name=name)
            nc.sync.dma_start(lst[:], src)
            return lst

        def load_words(name, words, tag=None):
            win = sb(name, [P, T], U32, tag)
            nc.sync.dma_start(win[:].bitcast(I32), words.rearrange("p t i -> p (t i)").bitcast(I32))
            return win

        def load_planes_side_by_side(plane, scales, passes):
            for r in range(4):
                nc.sync.dma_start(
                    plane[r:P:32, :].bitcast(I32).rearrange("q (a t) -> q a t", a=passes),
                    scales.bitcast(I32)[:, r:16:4, :].rearrange("a q t -> q a t"),
                )

        def load_scale_rows(name, scales, passes, first):
            rows = 16 * passes
            win = sb(name, [P, T], U8)
            words = win[:].bitcast(I32)
            nc.gpsimd.memset(words[0:first, :], 0)
            nc.gpsimd.memset(words[first + rows : P, :], 0)
            nc.sync.dma_start(words[first : first + rows, :], scales.bitcast(I32).rearrange("a q t -> q a t"))
            return win

        def deal_scale_rows(queue, plane, plane_row, picked, passes, first):
            rows = 4 * passes
            for q in range(QUADS):
                queue.dma_start(
                    plane[32 * q + plane_row : 32 * q + plane_row + 4, :].bitcast(I32),
                    picked[first + rows * q : first + rows * (q + 1), :].bitcast(I32),
                )

        def gather(name, dtype, window, offsets, tag=None):
            picked = sb(name, [P, S], dtype, tag)
            nc.vector.tensor_copy(picked[:], window.indirect(offsets[:]))
            return picked

        w4_scale = sb("w4_scale", [P, K_PASSES * H], U8)
        v_scale_win = sb("v_scale_win", [P, K_PASSES * T], U8)
        offer_scale = sb("offer_scale", [P, H_PASSES * 2 * S], U8)
        nc.vector.memset(v_scale_win[:].bitcast(I32), 0)
        nc.vector.memset(w4_scale[:].bitcast(I32), 0)
        nc.vector.memset(offer_scale[:].bitcast(I32), 0)

        idx = load_list("idx", offs)
        v_win = [load_words("v_win0", tab_words[0])]
        load_planes_side_by_side(v_scale_win, tab_scales, K_PASSES)
        w4_codes = sb("w4_codes", [P, K_PASSES, 2 * H], U8)
        nc.sync.dma_start(w4_codes[:].bitcast(I32), w4_words.bitcast(I32).rearrange("a p c -> p a c"))
        load_planes_side_by_side(w4_scale, w4_scales, K_PASSES)
        v_win.append(load_words("v_win1", tab_words[1]))
        v_win.append(load_words("v_win2", tab_words[2]))
        idx2 = load_list("idx2", offs2)
        v2_scale_win = load_scale_rows("v2_scale_win", tab2_scales, H_PASSES, OFFER_ROW)

        w1_raw = {}

        def w1_rows(a):
            return w1[a * PASS : (a + 1) * PASS, :].rearrange("(p i) c -> p i c", i=PACK)

        def load_w1(a, b):
            raw = sb("w1_raw%d_%d" % (a, b), [P, PACK, PASS], F32)
            nc.sync.dma_start(raw[:], w1_rows(a)[:, :, b * PASS : (b + 1) * PASS])
            w1_raw[a, b] = raw[:]

        load_w1(0, 0)
        idx3 = load_list("idx3", offs3)
        v3_scale_win = load_scale_rows("v3_scale_win", tab3_scales, H_PASSES, OFFER_ROW)
        steep_rows = sb("steep_rows", [P, P], F32)
        nc.gpsimd.memset(steep_rows[:], 0.0)
        nc.sync.dma_start(steep_rows[0:TILES, :], steep.rearrange("(c p) -> c p", p=P))
        for b in range(H_PASSES):
            for a in range(K_PASSES):
                if (a, b) != (0, 0):
                    load_w1(a, b)

        ident = sb("ident", [P, P], F32)
        make_identity(nc, ident[:])

        v_codes, v_scale = [], []
        for a in range(K_PASSES):
            v_codes.append(gather("v_codes%d" % a, U32, v_win[a][:], idx))
            v_scale.append(gather("v_scale%d" % a, U8, v_scale_win[:, a * T : (a + 1) * T], idx))
        v2_win = [load_words("v2_win%d" % b, tab2_words[b]) for b in range(H_PASSES)]
        offer_scale_rows = sb("offer_scale_rows", [P, 2 * S], U8)
        nc.vector.tensor_copy(offer_scale_rows[:, 0:S], v2_scale_win[:].indirect(idx2[:]))
        nc.vector.tensor_copy(offer_scale_rows[:, S : 2 * S], v3_scale_win[:].indirect(idx3[:]))
        deal_scale_rows(nc.sync, offer_scale, OFFER_PLANE, offer_scale_rows, H_PASSES, OFFER_ROW)
        v3_win = [load_words("v3_win0", tab3_words[0], "v3_scale_win")]
        h2_ps = [[bank(TILES * b + jt, "h2_ps%d_%d" % (b, jt)) for jt in range(TILES)] for b in range(H_PASSES)]
        for a in range(K_PASSES):
            for b in range(H_PASSES):
                for jt in range(TILES):
                    cols = slice(jt * P, (jt + 1) * P)
                    nc.tensor.matmul_mx(
                        out=h2_ps[b][jt][:],
                        lhsT=v_codes[a][:, cols].bitcast(FP8X4),
                        lhsT_scale=v_scale[a][:, cols],
                        rhs=w4_codes[:, a, 2 * b * PASS : 2 * (b + 1) * PASS].bitcast(FP4X4),
                        rhs_scale=w4_scale[:, a * H + b * PASS : a * H + (b + 1) * PASS],
                        start=(a == 0),
                        stop=(a == K_PASSES - 1),
                    )

        def by_word(ps):
            return ps[:].rearrange("j (p u e) -> j u p e", u=2, e=2)

        h2 = {}
        for b in range(H_PASSES):
            for jt in range(TILES):
                h2[b, jt] = sb("h2_%d_%d" % (b, jt), [P, 2, P, 2], F32)
                nc.scalar.copy(h2[b, jt][:], by_word(h2_ps[b][jt]))

        h1_ps = [[bank(TILES * b + jt, "h1_ps%d_%d" % (b, jt)) for jt in range(TILES)] for b in range(H_PASSES)]

        def round_w1(a, b, engines):
            width = PASS // len(engines)
            pieces = []
            for k, copy in enumerate(engines):
                name = "w1_bf%d_%d_%d" % (a, b, k)
                if len(engines) == 1:
                    grouped = ring("w1_bf", 3, name, [P, width, PACK], BF16)
                else:
                    grouped = sb(name, [P, width, PACK], BF16)
                copy(
                    grouped[:].rearrange("p (c n) i -> p c i n", n=2),
                    w1_raw[a, b][:, :, k * width : (k + 1) * width].rearrange("p i (c n) -> p c i n", n=2),
                )
                pieces.append(grouped)
            return pieces

        def quantise_w1_and_multiply(a, b, pieces):
            codes = sb("w1_codes%d_%d" % (a, b), [P, PASS], U32)
            scale = sb("w1_scale%d_%d" % (a, b), [P, PASS], U8)
            width = PASS // len(pieces)
            for k, grouped in enumerate(pieces):
                part = slice(k * width, (k + 1) * width)
                nc.vector.quantize_mx(
                    out=codes[:, part].bitcast(FP8X4),
                    scales=scale[:, part],
                    in_=grouped[:].rearrange("p c i -> p (c i)"),
                )
            for jt in range(TILES):
                cols = slice(jt * P, (jt + 1) * P)
                nc.tensor.matmul_mx(
                    out=h1_ps[b][jt][:],
                    lhsT=v_codes[a][:, cols].bitcast(FP8X4),
                    lhsT_scale=v_scale[a][:, cols],
                    rhs=codes[:].bitcast(FP8X4),
                    rhs_scale=scale[:],
                    start=(a == 0),
                    stop=(a == K_PASSES - 1),
                )


        def offer_plane(b, table, mt):
            lo = (2 * b + table) * S + mt * P
            return offer_scale[OFFER_PLANE:P, lo : lo + P]

        h_codes = [sb("h_codes%d" % b, [P, S], U32) for b in range(H_PASSES)]
        h_scale = [sb("h_scale%d" % b, [P, S], U8) for b in range(H_PASSES)]
        turn_banks = [[0, 1], [2, 3]]
        for b in range(H_PASSES):
            for a in range(K_PASSES):
                if a == K_PASSES - 1:
                    engines = [nc.vector.tensor_copy, nc.scalar.copy]
                else:
                    engines = [nc.vector.tensor_copy] if b == 0 else [nc.scalar.copy]
                quantise_w1_and_multiply(a, b, round_w1(a, b, engines))
                if (a, b) == (2, 0):
                    v3_win.append(load_words("v3_win1", tab3_words[1], "w1_raw2_0"))
            for jh in range(2):
                turned = bank(turn_banks[b][jh], "turned%d_%d" % (b, jh))
                turned_v = turned[:].rearrange("p (t u j) -> p t u j", t=2, u=2)
                hb = []
                for t in range(2):
                    jt = 2 * jh + t
                    if (b, jt) == (1, 2):
                        v2_codes = [gather("v2_codes0", U32, v2_win[0][:], idx2, "w1_bf2_1_1")]
                        h_bf = sb("h_bf1_2", [P, 2, P, 2], BF16, "v2_win0")
                    else:
                        h_bf = ring("h_bf", 4, "h_bf%d_%d" % (b, jt), [P, 2, P, 2], BF16)
                    nc.vector.tensor_tensor(h_bf[:], by_word(h1_ps[b][jt]), h2[b, jt][:], ALU.max)
                    hb.append(h_bf)
                for t in range(2):
                    words = hb[t][:].rearrange("j u p e -> j (u p e)").bitcast(F32)
                    for u in range(2):
                        nc.tensor.transpose(turned_v[:, t, u, :], words[:, u * P : (u + 1) * P], ident[:])
                h_grouped = sb("h_grouped%d_%d" % (b, jh), [P, HALF * PACK], BF16)
                nc.scalar.copy(
                    h_grouped[:].bitcast(F32).rearrange("p (t j u) -> p t j u", t=2, u=2),
                    turned[:].rearrange("p (t u j) -> p t j u", t=2, u=2),
                )
                if (b, jh) == (0, 1):
                    steep_ps = bank(3, "steep_ps")
                    nc.tensor.transpose(steep_ps[:, 0:P], steep_rows[:], ident[:])
                    steep_sb = sb("steep_sb", [P, TILES], F32)
                    nc.scalar.copy(steep_sb[:], steep_ps[:, 0:TILES])
                cols = slice(jh * HALF, (jh + 1) * HALF)
                nc.vector.quantize_mx(
                    out=h_codes[b][:, cols].bitcast(FP8X4), scales=h_scale[b][:, cols], in_=h_grouped[:]
                )
        v2_codes.append(gather("v2_codes1", U32, v2_win[1][:], idx2, "h_grouped1_0"))

        room = sb("room", [P, TILES, S], F32)
        room_banks = [[0, 1], [4, 5]]
        e2 = [[bank(room_banks[jh][mp], "e2_%d_%d" % (jh, mp)) for mp in range(2)] for jh in range(2)]
        for b in range(H_PASSES):
            for jh in range(2):
                cols = slice(jh * HALF, (jh + 1) * HALF)
                for mp in range(2):
                    for t in range(2):
                        mcols = slice((2 * mp + t) * P, (2 * mp + t + 1) * P)
                        nc.tensor.matmul_mx(
                            out=e2[jh][mp][:, t * HALF : (t + 1) * HALF],
                            lhsT=v2_codes[b][:, mcols].bitcast(FP8X4),
                            lhsT_scale=offer_plane(b, 0, 2 * mp + t),
                            rhs=h_codes[b][:, cols].bitcast(FP8X4),
                            rhs_scale=h_scale[b][:, cols],
                            start=(b == 0 and t == 0),
                            stop=(b == H_PASSES - 1 and t == 1),
                        )
                    if b == H_PASSES - 1:
                        nc.scalar.activation(
                            room[:, 2 * mp : 2 * mp + 2, cols],
                            e2[jh][mp][:].rearrange("m (t j) -> m t j", t=2),
                            ACT.Silu,
                        )

        mate_banks = [6, 7, 2, 3]
        e3 = [bank(mate_banks[mt], "e3_%d" % mt) for mt in range(TILES)]
        v3_codes = sb("v3_codes", [P, H_PASSES * S], U32, "h_grouped1_1")
        for mh in range(2):
            for b in range(H_PASSES):
                lo = mh * HALF
                nc.vector.tensor_copy(
                    v3_codes[:, b * S + lo : b * S + lo + HALF],
                    v3_win[b][:].indirect(idx3[:, lo // 16 : (lo + HALF) // 16]),
                )
                for mt in range(2 * mh, 2 * mh + 2):
                    nc.tensor.matmul_mx(
                        out=e3[mt][:],
                        lhsT=v3_codes[:, b * S + mt * P : b * S + (mt + 1) * P].bitcast(FP8X4),
                        lhsT_scale=offer_plane(b, 1, mt),
                        rhs=h_codes[b][:].bitcast(FP8X4),
                        rhs_scale=h_scale[b][:],
                        start=(b == 0),
                        stop=(b == H_PASSES - 1),
                    )
        for mt in range(TILES):
            score = sb("score%d" % mt, [P, S], F32)
            nc.scalar.activation(score[:], e3[mt][:], ACT.Tanh, scale=steep_sb[:, mt : mt + 1])
            nc.vector.tensor_tensor(score[:], score[:], room[:, mt, :], ALU.add)
            nc.sync.dma_start(out[mt * P : (mt + 1) * P, :], score[:])
